import numpy as np
import ml_dtypes

BF16 = ml_dtypes.bfloat16


def bf(x):
    return np.asarray(x, np.float32).astype(BF16)


def f32(x):
    return np.asarray(x, np.float32)


def f64(x):
    return np.asarray(x).astype(np.float64)


def striped(idx):
    return np.tile(idx.reshape(-1, 16).T, (8, 1))


def rows(idx, k):
    return np.tile(idx, (k, 1))


def look(tab, idx):
    return np.take_along_axis(f64(tab), rows(idx, len(tab)), axis=1)


K, S, D, V, N, M = 256, 2048, 2, 1024, 2048, 512


def setup_inputs():
    return {"tab": f32(np.random.standard_normal((2, K, S))), "t": f32(0.5 * np.random.standard_normal((K, V))), "w": bf(np.random.standard_normal((K, M)) / np.sqrt(K)), "b": f32(0.5 * np.random.standard_normal((M, 1))), "offs": striped(np.random.permutation(S)[:N])}


def reference(tab, t, w, b, offs):
    idx = offs[:16].T.reshape(-1)
    a = [look(tab[1], idx[d * V:(d + 1) * V]) + f64(t) for d in range(D)]
    e = [np.exp(np.maximum(v, 0.2 * v)) for v in a]
    x = sum(e[d] * look(tab[0], idx[d * V:(d + 1) * V]) for d in range(D)) / sum(e)
    return np.maximum(f64(w).T @ x + f64(b), 0.0)

@@ -1,0 +1,76 @@
+import concourse.mybir as mybir
+
+F32, BF16, U16 = mybir.dt.float32, mybir.dt.bfloat16, mybir.dt.uint16
+ALU = mybir.AluOpType
+ACT = mybir.ActivationFunctionType
+
+P = 128
+K, S, D, V, M = 256, 2048, 2, 1024, 512
+CHUNK = 512
+GROUP = 16
+SLOPE = 0.2
+FLOPS = 2 * K * M * V
+
+
+def tile_lookup_gat_relu_kernel(tc, tab, t, w, b, offs, out):
+    nc = tc.nc
+    blocks, chunks, outs = K // P, V // CHUNK, M // P
+    with (
+        tc.tile_pool(name="held", bufs=1) as held,
+        tc.tile_pool(name="work", bufs=2) as work,
+        tc.psum_pool(name="psum", bufs=8) as psum,
+    ):
+        offsets = held.tile([P, D * V // GROUP], U16, name="offsets")
+        nc.sync.dma_start(offsets[:], offs)
+        scores, values, own = [], [], []
+        for r in range(blocks):
+            rows = slice(r * P, (r + 1) * P)
+            scores.append(held.tile([P, S], F32, name=f"scores{r}"))
+            own.append(held.tile([P, V], F32, name=f"own{r}"))
+            nc.sync.dma_start(own[r][:], t[rows, :])
+            nc.sync.dma_start(scores[r][:], tab[1, rows, :])
+        for r in range(blocks):
+            values.append(held.tile([P, S], F32, name=f"values{r}"))
+            nc.sync.dma_start(values[r][:], tab[0, r * P:(r + 1) * P, :])
+        weights = held.tile([P, blocks, M], BF16, name="weights")
+        nc.sync.dma_start(weights[:], w.rearrange("(r p) m -> p r m", p=P))
+        bias = held.tile([P, outs], F32, name="bias")
+        nc.sync.dma_start(bias[:], b.rearrange("(p q) o -> p (q o)", q=outs))
+        out_rows = out.rearrange("(p q) j -> p q j", q=outs)
+
+        def entries(d, c):
+            first = (d * V + c * CHUNK) // GROUP
+            return offsets[:, first:first + CHUNK // GROUP]
+
+        share = {}
+        for r in range(blocks):
+            for c in range(chunks):
+                cols = slice(c * CHUNK, (c + 1) * CHUNK)
+                leaky = []
+                for d in range(D):
+                    a = work.tile([P, CHUNK], F32, name=f"a{d}")
+                    nc.vector.tensor_tensor(a[:], scores[r][:].indirect(entries(d, c)), own[r][:, cols], ALU.add)
+                    leaky.append(work.tile([P, CHUNK], F32, name=f"leaky{d}"))
+                    nc.vector.scalar_tensor_tensor(leaky[d][:], a[:], SLOPE, a[:], ALU.mult, ALU.max)
+                gap = work.tile([P, CHUNK], F32, name="gap")
+                nc.vector.tensor_tensor(gap[:], leaky[0][:], leaky[1][:], ALU.subtract)
+                for d, sign in enumerate((1.0, -1.0)):
+                    share[r, c, d] = held.tile([P, CHUNK], F32, name=f"share{r}{c}{d}")
+                    nc.scalar.activation(share[r, c, d][:], gap[:], ACT.Sigmoid, scale=sign)
+
+        for c in range(chunks):
+            x = []
+            for r in range(blocks):
+                parts = []
+                for d in range(D):
+                    parts.append(work.tile([P, CHUNK], F32, name=f"part{d}"))
+                    nc.vector.tensor_tensor(parts[d][:], values[r][:].indirect(entries(d, c)), share[r, c, d][:], ALU.mult)
+                x.append(work.tile([P, CHUNK], BF16, name=f"x{r}"))
+                nc.vector.tensor_tensor(x[r][:], parts[0][:], parts[1][:], ALU.add)
+            for q in range(outs):
+                layer = psum.tile([P, CHUNK], F32, name="layer")
+                for r in range(blocks):
+                    nc.tensor.matmul(layer[:], weights[:, r, q::outs], x[r][:], start=(r == 0), stop=(r == blocks - 1))
+                result = held.tile([P, CHUNK], F32, name=f"result{c}{q}")
+                nc.scalar.activation(result[:], layer[:], ACT.Relu, bias=bias[:, q:q + 1])
+                nc.sync.dma_start(out_rows[:, q, c * CHUNK:(c + 1) * CHUNK], result[:])

@@ -1,4 +1,5 @@
 import concourse.mybir as mybir
+from concourse.masks import make_identity
 
 F32, BF16, U16 = mybir.dt.float32, mybir.dt.bfloat16, mybir.dt.uint16
 ALU = mybir.AluOpType
@@ -7,6 +8,7 @@ ACT = mybir.ActivationFunctionType
 P = 128
 K, S, D, V, M = 256, 2048, 2, 1024, 512
 CHUNK = 512
+WIDTHS = (512, 256, 256)
 GROUP = 16
 SLOPE = 0.2
 FLOPS = 2 * K * M * V
@@ -17,18 +19,20 @@ def tile_lookup_gat_relu_kernel(tc, tab, t, w, b, offs, out):
     blocks, chunks, outs = K // P, V // CHUNK, M // P
     with (
         tc.tile_pool(name="held", bufs=1) as held,
-        tc.tile_pool(name="work", bufs=2) as work,
+        tc.tile_pool(name="work", bufs=4) as work,
         tc.psum_pool(name="psum", bufs=8) as psum,
     ):
         offsets = held.tile([P, D * V // GROUP], U16, name="offsets")
         nc.sync.dma_start(offsets[:], offs)
-        scores, values, own = [], [], []
-        for r in range(blocks):
-            rows = slice(r * P, (r + 1) * P)
-            scores.append(held.tile([P, S], F32, name=f"scores{r}"))
-            own.append(held.tile([P, V], F32, name=f"own{r}"))
-            nc.sync.dma_start(own[r][:], t[rows, :])
-            nc.sync.dma_start(scores[r][:], tab[1, rows, :])
+        scores, values, own = [], [], {}
+        for c in range(chunks):
+            for r in range(blocks):
+                rows = slice(r * P, (r + 1) * P)
+                if c == 0:
+                    scores.append(held.tile([P, S], F32, name=f"scores{r}"))
+                    nc.sync.dma_start(scores[r][:], tab[1, rows, :])
+                own[r, c] = held.tile([P, CHUNK], F32, name=f"own{r}{c}")
+                nc.sync.dma_start(own[r, c][:], t[rows, c * CHUNK:(c + 1) * CHUNK])
         for r in range(blocks):
             values.append(held.tile([P, S], F32, name=f"values{r}"))
             nc.sync.dma_start(values[r][:], tab[0, r * P:(r + 1) * P, :])
@@ -38,39 +42,53 @@ def tile_lookup_gat_relu_kernel(tc, tab, t, w, b, offs, out):
         nc.sync.dma_start(bias[:], b.rearrange("(p q) o -> p (q o)", q=outs))
         out_rows = out.rearrange("(p q) j -> p q j", q=outs)
 
-        def entries(d, c):
-            first = (d * V + c * CHUNK) // GROUP
-            return offsets[:, first:first + CHUNK // GROUP]
+        plus = held.tile([P, P], F32, name="plus")
+        make_identity(nc, plus[:])
+        minus = held.tile([P, P], F32, name="minus")
+        nc.scalar.mul(minus[:], plus[:], -1.0)
+
+        def entries(d, first, count):
+            column = (d * V + first) // GROUP
+            return offsets[:, column:column + count // GROUP]
 
         share = {}
-        for r in range(blocks):
-            for c in range(chunks):
-                cols = slice(c * CHUNK, (c + 1) * CHUNK)
-                leaky = []
+        for c in range(chunks):
+            for r in range(blocks):
+                logit, bend = [], []
                 for d in range(D):
-                    a = work.tile([P, CHUNK], F32, name=f"a{d}")
-                    nc.vector.tensor_tensor(a[:], scores[r][:].indirect(entries(d, c)), own[r][:, cols], ALU.add)
-                    leaky.append(work.tile([P, CHUNK], F32, name=f"leaky{d}"))
-                    nc.vector.scalar_tensor_tensor(leaky[d][:], a[:], SLOPE, a[:], ALU.mult, ALU.max)
-                gap = work.tile([P, CHUNK], F32, name="gap")
-                nc.vector.tensor_tensor(gap[:], leaky[0][:], leaky[1][:], ALU.subtract)
+                    logit.append(work.tile([P, CHUNK], F32, name=f"logit{d}"))
+                    nc.vector.tensor_tensor(logit[d][:], scores[r][:].indirect(entries(d, c * CHUNK, CHUNK)), own[r, c][:], ALU.add)
+                    bend.append(work.tile([P, CHUNK], F32, name=f"bend{d}"))
+                    nc.scalar.activation(bend[d][:], logit[d][:], ACT.Relu, scale=(1.0 - SLOPE) / SLOPE)
+                straight = work.tile([P, CHUNK], F32, name="straight")
+                nc.vector.tensor_tensor(straight[:], logit[0][:], logit[1][:], ALU.subtract)
+                gap = psum.tile([P, CHUNK], F32, name="gap", tag="bank")
+                nc.tensor.matmul(gap[:], plus[:], bend[0][:], start=True, stop=False)
+                nc.tensor.matmul(gap[:], minus[:], bend[1][:], start=False, stop=False)
+                nc.tensor.matmul(gap[:], plus[:], straight[:], start=False, stop=True)
                 for d, sign in enumerate((1.0, -1.0)):
                     share[r, c, d] = held.tile([P, CHUNK], F32, name=f"share{r}{c}{d}")
-                    nc.scalar.activation(share[r, c, d][:], gap[:], ACT.Sigmoid, scale=sign)
+                    nc.scalar.activation(share[r, c, d][:], gap[:], ACT.Sigmoid, scale=sign * SLOPE)
 
-        for c in range(chunks):
-            x = []
+        start = 0
+        for n, width in enumerate(WIDTHS):
+            c, first = divmod(start, CHUNK)
+            layer = [psum.tile([P, width], F32, name="layer", tag="bank") for q in range(outs)]
             for r in range(blocks):
                 parts = []
                 for d in range(D):
-                    parts.append(work.tile([P, CHUNK], F32, name=f"part{d}"))
-                    nc.vector.tensor_tensor(parts[d][:], values[r][:].indirect(entries(d, c)), share[r, c, d][:], ALU.mult)
-                x.append(work.tile([P, CHUNK], BF16, name=f"x{r}"))
-                nc.vector.tensor_tensor(x[r][:], parts[0][:], parts[1][:], ALU.add)
+                    parts.append(work.tile([P, width], F32, name=f"part{d}"))
+                    nc.vector.tensor_tensor(parts[d][:], values[r][:].indirect(entries(d, start, width)),
+                                            share[r, c, d][:, first:first + width], ALU.mult)
+                x = work.tile([P, width], BF16, name=f"x{r}")
+                nc.vector.tensor_tensor(x[:], parts[0][:], parts[1][:], ALU.add)
+                for q in range(outs):
+                    nc.tensor.matmul(layer[q][:], weights[:, r, q::outs], x[:], start=(r == 0), stop=(r == blocks - 1))
             for q in range(outs):
-                layer = psum.tile([P, CHUNK], F32, name="layer")
-                for r in range(blocks):
-                    nc.tensor.matmul(layer[:], weights[:, r, q::outs], x[r][:], start=(r == 0), stop=(r == blocks - 1))
-                result = held.tile([P, CHUNK], F32, name=f"result{c}{q}")
-                nc.scalar.activation(result[:], layer[:], ACT.Relu, bias=bias[:, q:q + 1])
-                nc.sync.dma_start(out_rows[:, q, c * CHUNK:(c + 1) * CHUNK], result[:])
+                result = held.tile([P, width], F32, name=f"result{n}{q}")
+                if n == len(WIDTHS) - 1 and q % 2 == 1:
+                    nc.vector.tensor_scalar(result[:], layer[q][:], bias[:, q:q + 1], 0.0, ALU.add, ALU.max)
+                else:
+                    nc.scalar.activation(result[:], layer[q][:], ACT.Relu, bias=bias[:, q:q + 1])
+                nc.sync.dma_start(out_rows[:, q, start:start + width], result[:])
+            start += width

@@ -28,11 +28,11 @@ def tile_lookup_gat_relu_kernel(tc, tab, t, w, b, offs, out):
         for c in range(chunks):
             for r in range(blocks):
                 rows = slice(r * P, (r + 1) * P)
+                own[r, c] = held.tile([P, CHUNK], F32, name=f"own{r}{c}")
+                nc.sync.dma_start(own[r, c][:], t[rows, c * CHUNK:(c + 1) * CHUNK])
                 if c == 0:
                     scores.append(held.tile([P, S], F32, name=f"scores{r}"))
                     nc.sync.dma_start(scores[r][:], tab[1, rows, :])
-                own[r, c] = held.tile([P, CHUNK], F32, name=f"own{r}{c}")
-                nc.sync.dma_start(own[r, c][:], t[rows, c * CHUNK:(c + 1) * CHUNK])
         for r in range(blocks):
             values.append(held.tile([P, S], F32, name=f"values{r}"))
             nc.sync.dma_start(values[r][:], tab[0, r * P:(r + 1) * P, :])
@@ -44,6 +44,9 @@ def tile_lookup_gat_relu_kernel(tc, tab, t, w, b, offs, out):
 
         plus = held.tile([P, P], F32, name="plus")
         make_identity(nc, plus[:])
+        idle = psum.tile([P, CHUNK], F32, name="idle", tag="bank")
+        for k in range(2):
+            nc.tensor.matmul(idle[:], plus[:], own[0, 0][:], start=True, stop=True)
         minus = held.tile([P, P], F32, name="minus")
         nc.scalar.mul(minus[:], plus[:], -1.0)
 
@@ -58,7 +61,7 @@ def tile_lookup_gat_relu_kernel(tc, tab, t, w, b, offs, out):
                 for d in range(D):
                     logit.append(work.tile([P, CHUNK], F32, name=f"logit{d}"))
                     nc.vector.tensor_tensor(logit[d][:], scores[r][:].indirect(entries(d, c * CHUNK, CHUNK)), own[r, c][:], ALU.add)
-                    bend.append(work.tile([P, CHUNK], F32, name=f"bend{d}"))
+                    bend.append(work.tile([P, CHUNK], F32, name=f"bend{d}", bufs=2))
                     nc.scalar.activation(bend[d][:], logit[d][:], ACT.Relu, scale=(1.0 - SLOPE) / SLOPE)
                 straight = work.tile([P, CHUNK], F32, name="straight")
                 nc.vector.tensor_tensor(straight[:], logit[0][:], logit[1][:], ALU.subtract)

import concourse.mybir as mybir
from concourse.masks import make_identity

F32, BF16, U16 = mybir.dt.float32, mybir.dt.bfloat16, mybir.dt.uint16
ALU = mybir.AluOpType
ACT = mybir.ActivationFunctionType

P = 128
K, S, D, V, M = 256, 2048, 2, 1024, 512
CHUNK = 512
WIDTHS = (512, 256, 256)
GROUP = 16
SLOPE = 0.2
FLOPS = 2 * K * M * V


def tile_lookup_gat_relu_kernel(tc, tab, t, w, b, offs, out):
    nc = tc.nc
    blocks, chunks, outs = K // P, V // CHUNK, M // P
    with (
        tc.tile_pool(name="held", bufs=1) as held,
        tc.tile_pool(name="work", bufs=4) as work,
        tc.psum_pool(name="psum", bufs=8) as psum,
    ):
        offsets = held.tile([P, D * V // GROUP], U16, name="offsets")
        nc.sync.dma_start(offsets[:], offs)
        scores, values, own = [], [], {}
        for c in range(chunks):
            for r in range(blocks):
                rows = slice(r * P, (r + 1) * P)
                own[r, c] = held.tile([P, CHUNK], F32, name=f"own{r}{c}")
                nc.sync.dma_start(own[r, c][:], t[rows, c * CHUNK:(c + 1) * CHUNK])
                if c == 0:
                    scores.append(held.tile([P, S], F32, name=f"scores{r}"))
                    nc.sync.dma_start(scores[r][:], tab[1, rows, :])
        for r in range(blocks):
            values.append(held.tile([P, S], F32, name=f"values{r}"))
            nc.sync.dma_start(values[r][:], tab[0, r * P:(r + 1) * P, :])
        weights = held.tile([P, blocks, M], BF16, name="weights")
        nc.sync.dma_start(weights[:], w.rearrange("(r p) m -> p r m", p=P))
        bias = held.tile([P, outs], F32, name="bias")
        nc.sync.dma_start(bias[:], b.rearrange("(p q) o -> p (q o)", q=outs))
        out_rows = out.rearrange("(p q) j -> p q j", q=outs)

        plus = held.tile([P, P], F32, name="plus")
        make_identity(nc, plus[:])
        idle = psum.tile([P, CHUNK], F32, name="idle", tag="bank")
        for k in range(2):
            nc.tensor.matmul(idle[:], plus[:], own[0, 0][:], start=True, stop=True)
        minus = held.tile([P, P], F32, name="minus")
        nc.scalar.mul(minus[:], plus[:], -1.0)

        def entries(d, first, count):
            column = (d * V + first) // GROUP
            return offsets[:, column:column + count // GROUP]

        share = {}
        for c in range(chunks):
            for r in range(blocks):
                logit, bend = [], []
                for d in range(D):
                    logit.append(work.tile([P, CHUNK], F32, name=f"logit{d}"))
                    nc.vector.tensor_tensor(logit[d][:], scores[r][:].indirect(entries(d, c * CHUNK, CHUNK)), own[r, c][:], ALU.add)
                    bend.append(work.tile([P, CHUNK], F32, name=f"bend{d}", bufs=2))
                    nc.scalar.activation(bend[d][:], logit[d][:], ACT.Relu, scale=(1.0 - SLOPE) / SLOPE)
                straight = work.tile([P, CHUNK], F32, name="straight")
                nc.vector.tensor_tensor(straight[:], logit[0][:], logit[1][:], ALU.subtract)
                gap = psum.tile([P, CHUNK], F32, name="gap", tag="bank")
                nc.tensor.matmul(gap[:], plus[:], bend[0][:], start=True, stop=False)
                nc.tensor.matmul(gap[:], minus[:], bend[1][:], start=False, stop=False)
                nc.tensor.matmul(gap[:], plus[:], straight[:], start=False, stop=True)
                for d, sign in enumerate((1.0, -1.0)):
                    share[r, c, d] = held.tile([P, CHUNK], F32, name=f"share{r}{c}{d}")
                    nc.scalar.activation(share[r, c, d][:], gap[:], ACT.Sigmoid, scale=sign * SLOPE)

        start = 0
        for n, width in enumerate(WIDTHS):
            c, first = divmod(start, CHUNK)
            layer = [psum.tile([P, width], F32, name="layer", tag="bank") for q in range(outs)]
            for r in range(blocks):
                parts = []
                for d in range(D):
                    parts.append(work.tile([P, width], F32, name=f"part{d}"))
                    nc.vector.tensor_tensor(parts[d][:], values[r][:].indirect(entries(d, start, width)),
                                            share[r, c, d][:, first:first + width], ALU.mult)
                x = work.tile([P, width], BF16, name=f"x{r}")
                nc.vector.tensor_tensor(x[:], parts[0][:], parts[1][:], ALU.add)
                for q in range(outs):
                    nc.tensor.matmul(layer[q][:], weights[:, r, q::outs], x[:], start=(r == 0), stop=(r == blocks - 1))
            for q in range(outs):
                result = held.tile([P, width], F32, name=f"result{n}{q}")
                if n == len(WIDTHS) - 1 and q % 2 == 1:
                    nc.vector.tensor_scalar(result[:], layer[q][:], bias[:, q:q + 1], 0.0, ALU.add, ALU.max)
                else:
                    nc.scalar.activation(result[:], layer[q][:], ACT.Relu, bias=bias[:, q:q + 1])
                nc.sync.dma_start(out_rows[:, q, start:start + width], result[:])
            start += width
